import numpy as np, ml_dtypes
CORES = [2,6,10,14,18,22,26,30]
N = 8
import mx_ref
BF = ml_dtypes.bfloat16
def entries(a):
    return np.ascontiguousarray(a.T).reshape(-1)
def table(e):
    return np.ascontiguousarray(np.reshape(e, (-1, 16)).T).astype(np.int32)
def cols(t, e):
    v = np.concatenate([t.reshape(128, -1, 4), np.zeros((128, 1, 4), BF)], axis=1)
    return np.ascontiguousarray(v[:, e]).reshape(128, -1)
def tile(rs):
    return np.stack(rs, axis=2).reshape(128, -1).astype(BF)
def cut(t, i, w=512):
    return t[:, w * i:w * i + w]
def f(rng, *shape):
    return mx_ref.flush((rng.standard_normal(shape, dtype=np.float32) * np.exp2(rng.integers(-2, 3, shape[:-1] + (1,)))).astype(BF))
def wide(rng, *shape, cols=0):
    v = rng.standard_normal(shape, dtype=np.float32) * np.exp2(rng.integers(-12, 13, shape)).astype(np.float32)
    if cols: v *= np.repeat(np.exp2(rng.integers(-cols, cols + 1, shape[:-2] + (1, shape[-1] // 4))) * (rng.random(shape[:-2] + (1, shape[-1] // 4)) > 0.0625), 4, axis=-1).astype(np.float32)
    return mx_ref.flush(v.astype(BF))
T, P, CAPP = 256, 128, 16
BASE = T + 3 * P
def sends(a):
    return entries(a).reshape(3, N, CAPP)
def filled(s, r, t):
    return s[:, :t, r].transpose(1, 0, 2).reshape(-1) >= 0
def lists(rng, how=""):
    s = np.full((N, 3, N, CAPP), -1)
    a = int(rng.integers(0, N)); same = (a, int(rng.integers(0, 3)), (a + int(rng.integers(1, N))) % N)
    for t in range(3):
        for q in range(N):
            got = BASE + np.flatnonzero(filled(s, q, t))
            for r in range(N):
                if q == r: continue
                least = 1 if t == 0 and r == (q + 1) % N else 0
                k = rng.permutation(CAPP)[:CAPP if how == "far" else rng.integers(least, CAPP + 1)]
                e = rng.integers(T + (t - 1) * P if how == "far" and t > 0 else 0, T + t * P, len(k))
                if t > 0:
                    m = (len(k) + 1) // 2; e[:m] = got[rng.integers(0, len(got), m)]
                s[q, t, r, k] = e
                if how == "shared" and (q, t, r) == same: s[q, t, r] = rng.integers(0, T + t * P)
    c = np.zeros((N, 2, 3, P), int)
    for r in range(N):
        for t in range(3):
            low = 2 if how == "skip" and t == 2 else t + 1
            own = T + (low - 1) * P; got = BASE + np.flatnonzero(filled(s, r, low))
            for h in range(2):
                c[r, h, t] = rng.integers(0, own, P)
                if len(got):
                    there = np.ones(P, bool) if how == "far" else rng.random(P) < 0.5
                    c[r, h, t] = np.where(there, got[rng.integers(0, len(got), P)], c[r, h, t])
            if how == "shared":
                one = int(c[r, 0, t, 0]); k = rng.permutation(P)
                c[r, 0, t, k[:P - P // 8]] = one; c[r, 1, t, k[:P // 8]] = one
            if how == "chains":
                c[r, 0, t] = np.arange(P) % T if t == 0 else T + (t - 1) * P + np.arange(P)
                c[r, 1, t] = rng.integers(0, T, P)
    return {"sn": np.stack([table(s[r]) for r in range(N)]), "lc": np.stack([table(c[r, 0]) for r in range(N)]), "rc": np.stack([table(c[r, 1]) for r in range(N)])}
def setup_inputs(rng):
    return {"x": f(rng, N, 128, 4 * T), "wl": np.stack([f(rng, 128, 2048)] * N), "wr": np.stack([f(rng, 128, 2048)] * N), "v": f(rng, N, 128, 512), **lists(rng)}
def setup_inputs_chains(rng):
    return {**setup_inputs(rng), **lists(rng, "chains")}
def setup_inputs_far(rng):
    return {**setup_inputs(rng), **lists(rng, "far")}
def setup_inputs_shared(rng):
    return {**setup_inputs(rng), **lists(rng, "shared")}
def setup_inputs_skip(rng):
    return {**setup_inputs(rng), **lists(rng, "skip")}
def setup_inputs_spread(rng):
    d = setup_inputs(rng); d["x"] = wide(rng, N, 128, 4 * T, cols=8); return d
def check_inputs(d):
    b = []
    for n in ("wl", "wr"):
        if any((d[n][r] != d[n][0]).any() for r in range(N)): b.append(n)
    s = np.stack([sends(d["sn"][r]) for r in range(N)])
    for r in range(N):
        for t in range(3):
            own = np.concatenate([np.ones(T + t * P, bool), np.zeros((3 - t) * P, bool)])
            ok = np.concatenate([own, filled(s, r, t)]); e = s[r, t]
            if e.min() < -1 or e.max() >= len(ok) or not ok[e[e >= 0]].all() or (s[r, t, r] != -1).any(): b.append("sn")
            ok = np.concatenate([own, filled(s, r, t + 1)])
            for n in ("lc", "rc"):
                e = entries(d[n][r])[t * P:t * P + P]
                if e.min() < 0 or e.max() >= len(ok) or not ok[e].all(): b.append(n)
    return b
def reference(x, wl, wr, v, sn, lc, rc):
    WL = [[mx_ref.quantize(np.ascontiguousarray(cut(wl[r], i))) for i in range(4)] for r in range(N)]
    WR = [[mx_ref.quantize(np.ascontiguousarray(cut(wr[r], i))) for i in range(4)] for r in range(N)]
    pool = [x[r] for r in range(N)]; slots = [[] for r in range(N)]
    for t in range(3):
        before = [np.concatenate([pool[r], np.zeros((128, 4 * (3 - t) * P), BF)] + slots[r], axis=1) for r in range(N)]
        for r in range(N):
            for q in range(N): slots[r].append(cols(before[q], sends(sn[q])[t, r]))
        made = []
        for r in range(N):
            known = np.concatenate([before[r]] + slots[r][t * N:], axis=1)
            left = mx_ref.quantize(cols(known, entries(lc[r])[t * P:t * P + P]))
            right = mx_ref.quantize(cols(known, entries(rc[r])[t * P:t * P + P]))
            made.append(tile([np.maximum(mx_ref.matmul(WL[r][i], left) + mx_ref.matmul(WR[r][i], right), np.float32(0)) * np.float32(0.05) for i in range(4)]))
        pool = [np.concatenate([pool[r], made[r]], axis=1) for r in range(N)]
    y = np.zeros((N, 128, P), np.float32)
    for r in range(N):
        y[r] = mx_ref.matmul(mx_ref.quantize(v[r]), mx_ref.quantize(np.ascontiguousarray(pool[r][:, 4 * (T + 2 * P):])))
    return {"y": y}

@@ -1,0 +1,232 @@
+from concourse.bass import DstId, RemoteDMATransfer
+from concourse.mybir import dt, AluOpType, ActivationFunctionType
+
+N, LEAVES, P, CAPP = 8, 256, 128, 16
+BASE = LEAVES + 3 * P
+SLOTS = N * CAPP
+L = (1, 2, 3)
+
+SCRATCH = {
+    "xt": ("sbuf", [128, 4 * LEAVES], "bfloat16"),
+    "wlt": ("sbuf", [128, 2048], "bfloat16"),
+    "wrt": ("sbuf", [128, 2048], "bfloat16"),
+    "vt": ("sbuf", [128, 512], "bfloat16"),
+    "wlq": ("sbuf", [128, 512], "float8_e4m3fn_x4"),
+    "wls": ("sbuf", [128, 512], "uint8"),
+    "wrq": ("sbuf", [128, 512], "float8_e4m3fn_x4"),
+    "wrs": ("sbuf", [128, 512], "uint8"),
+    "vq": ("sbuf", [128, 128], "float8_e4m3fn_x4"),
+    "vs": ("sbuf", [128, 128], "uint8"),
+    "sni": ("sbuf", [128, 24], "int32"),
+    "sno": ("sbuf", [128, 24], "uint16"),
+    "lri": ("sbuf", [128, 48], "int32"),
+    "lro": ("sbuf", [128, 48], "uint16"),
+    "ida": ("sbuf", [128, 8], "int32"),
+    "idb": ("sbuf", [128, 8], "int32"),
+    "idc": ("sbuf", [128, 8], "int32"),
+    "idd": ("sbuf", [128, 8], "int32"),
+    "idu": ("sbuf", [128, 8], "uint16"),
+    "w1q": ("sbuf", [128, LEAVES], "float8_e4m3fn_x4"),
+    "w1s": ("sbuf", [128, LEAVES], "uint8"),
+    "hq": ("sbuf", [128, P], "float8_e4m3fn_x4"),
+    "hs": ("sbuf", [128, P], "uint8"),
+    "ysb": ("sbuf", [128, P], "float32"),
+    "ps": ("psum", [128, 2048], "float32"),
+    "psy": ("psum", [128, 512], "float32"),
+}
+SEMAPHORES = ["ldx", "ldsn", "ldwl", "ldwr", "ldlr", "ldv", "csn", "clr", "q1", "qwl", "qwr", "qv",
+              "iot", "id1", "id2", "idf", "fill2", "fill3", "fill4", "sent", "qh", "mmy", "ycp", "sty"]
+for t in L:
+    SCRATCH["w%dq" % (t + 1)] = ("sbuf", [128, BASE + t * SLOTS], "float8_e4m3fn_x4")
+    SCRATCH["w%ds" % (t + 1)] = ("sbuf", [128, BASE + t * SLOTS], "uint8")
+    for b in ("s", "a", "b"):
+        SCRATCH["%s%dq" % (b, t)] = ("sbuf", [128, 128], "float8_e4m3fn_x4")
+        SCRATCH["%s%ds" % (b, t)] = ("sbuf", [128, 128], "uint8")
+    SCRATCH["h%d" % t] = ("sbuf", [128, 4 * P], "bfloat16")
+    SEMAPHORES += ["%s%d" % (n, t) for n in ("pc", "pp", "arc", "ars", "ac", "as", "bc", "bs",
+                                             "m0_", "m1_", "m2_", "m3_", "ev", "nd")]
+
+
+def plan(src, cores, topo):
+    away = [d for d in cores if topo.chip(d) != topo.chip(src)]
+    home = [d for d in cores if topo.chip(d) == topo.chip(src) and d != src]
+    off = topo.engines(src, away[0])
+    half = len(off) // 2
+    codes, scales = {}, {}
+    for k, d in enumerate(away):
+        if k < 2:
+            codes[d] = off[2 * k:2 * k + 2]
+            scales[d] = off[half + 2 * k:half + 2 * k + 2]
+        else:
+            codes[d] = [off[half + k - 2]]
+            scales[d] = [off[k - 2]]
+    for k, d in enumerate(home):
+        own = [e for e in topo.engines(src, d) if e not in off]
+        codes[d] = scales[d] = own[2 * k:2 * k + 2]
+    return codes, scales
+
+
+def rank_program(g, core, T, topo):
+    rank = T.rank_of(core)
+    if rank is None:
+        return
+    cores = list(T.cores)
+    sem = T.sem
+    ve, sc, te, sy = g.vector, g.scalar, g.tensor, g.sync
+    Copy, Relu = ActivationFunctionType.Copy, ActivationFunctionType.Relu
+
+    def pick_codes(out, o0, o1, win, w0, w1, off, i0, i1):
+        return ve.tensor_copy(T[out][:, o0:o1].bitcast(dt.uint32),
+                              T[win][:, w0:w1].bitcast(dt.uint32).indirect(T[off][:, i0:i1]))
+
+    def pick_scales_v(out, o0, o1, win, w0, w1, off, i0, i1):
+        return ve.tensor_copy(T[out][:, o0:o1], T[win][:, w0:w1].indirect(T[off][:, i0:i1]))
+
+    def pick_scales_s(out, o0, o1, win, w0, w1, off, i0, i1):
+        return sc.activation(T[out][:, o0:o1], T[win][:, w0:w1].indirect(T[off][:, i0:i1]), Copy)
+
+    sc.dma_start(T.xt[:], T.x[:]).then_inc(sem.ldx, 16)
+    for k in range(8):
+        (sy if k % 2 == 0 else sc).dma_start(T.sni[16 * k:16 * k + 16, :], T.sn[:]).then_inc(sem.ldsn, 16)
+    sy.dma_start(T.wlt[:], T.wl[:]).then_inc(sem.ldwl, 16)
+    sy.dma_start(T.wrt[:], T.wr[:]).then_inc(sem.ldwr, 16)
+    for k in range(8):
+        sy.dma_start(T.lri[16 * k:16 * k + 16, 0:24], T.lc[:]).then_inc(sem.ldlr, 16)
+        sy.dma_start(T.lri[16 * k:16 * k + 16, 24:48], T.rc[:]).then_inc(sem.ldlr, 16)
+    sy.dma_start(T.vt[:], T.v[:]).then_inc(sem.ldv, 16)
+
+    g.iota(T.ida[:], [[0, 8]], 0, 1).then_inc(sem.iot, 1)
+    n_iota = 1
+    for a, b, base in ((0, rank, 0), (rank, rank + 1, 16 * ((rank + 1) % N)), (rank + 1, N, 16 * (rank + 1))):
+        if a < b:
+            g.iota(T.idb[:, a:b], [[16, b - a]], base, 0).then_inc(sem.iot, 1)
+            n_iota += 1
+
+    ve.wait_ge(sem.ldsn, 128)
+    ve.tensor_copy(T.sno[:], T.sni[:]).then_inc(sem.csn, 1)
+    ve.wait_ge(sem.ldx, 16)
+    ve.quantize_mx(T.w1q[:], T.w1s[:], T.xt[:]).then_inc(sem.q1, 1)
+    ve.wait_ge(sem.csn, 1)
+    ve.wait_ge(sem.q1, 1)
+    pick_codes("s1q", 0, 128, "w1q", 0, LEAVES, "sno", 0, 8).then_inc(sem.pc1, 1)
+    sc.wait_ge(sem.csn, 1)
+    sc.wait_ge(sem.q1, 1)
+    pick_scales_s("s1s", 0, 128, "w1s", 0, LEAVES, "sno", 0, 8).then_inc(sem.pp1, 1)
+
+    ve.quantize_mx(T.w2q[:, 0:LEAVES], T.w2s[:, 0:LEAVES], T.xt[:]).then_inc(sem.fill2, 1)
+    ve.wait_ge(sem.iot, n_iota)
+    ve.tensor_scalar(T.idc[:], T.ida[:], 15, None, AluOpType.bitwise_and).then_inc(sem.id1, 1)
+    ve.wait_ge(sem.id1, 1)
+    ve.tensor_tensor(T.idd[:], T.idc[:], T.idb[:], AluOpType.add).then_inc(sem.id2, 1)
+    ve.wait_ge(sem.id2, 1)
+    ve.tensor_copy(T.idu[:], T.idd[:]).then_inc(sem.idf, 1)
+    ve.wait_ge(sem.ldwl, 16)
+    ve.quantize_mx(T.wlq[:], T.wls[:], T.wlt[:]).then_inc(sem.qwl, 1)
+    ve.wait_ge(sem.ldwr, 16)
+    ve.quantize_mx(T.wrq[:], T.wrs[:], T.wrt[:]).then_inc(sem.qwr, 1)
+    ve.wait_ge(sem.ldlr, 256)
+    ve.tensor_copy(T.lro[:], T.lri[:]).then_inc(sem.clr, 1)
+    ve.quantize_mx(T.w3q[:, 0:LEAVES], T.w3s[:, 0:LEAVES], T.xt[:]).then_inc(sem.fill3, 1)
+    ve.quantize_mx(T.w4q[:, 0:LEAVES], T.w4s[:, 0:LEAVES], T.xt[:]).then_inc(sem.fill4, 1)
+    ve.wait_ge(sem.ldv, 16)
+    ve.quantize_mx(T.vq[:], T.vs[:], T.vt[:]).then_inc(sem.qv, 1)
+    ve.wait_ge(sem.clr, 1)
+    ve.wait_ge(sem.idf, 1)
+    sc.wait_ge(sem.clr, 1)
+    sc.wait_ge(sem.idf, 1)
+    te.wait_ge(sem.qwl, 1)
+    te.wait_ge(sem.qwr, 1)
+    te.wait_ge(sem.qv, 1)
+
+    plans = {c: plan(c, cores, topo) for c in cores}
+    expect_c = sum(len(plans[c][0][core]) for c in cores if c != core)
+    expect_s = sum(len(plans[c][1][core]) for c in cores if c != core)
+    n_sent = 0
+
+    def send(t, kind):
+        part, letter = plans[core][0 if kind == "c" else 1], "q" if kind == "c" else "s"
+        lo = BASE + ((t - 1) * N + rank) * CAPP
+        moves = []
+        for d in sorted(part, key=lambda c: (topo.chip(c) == topo.chip(core), c)):
+            q = T.rank_of(d)
+            rid, pid, _ = topo.addr(d)
+            src = T["s%d%s" % (t, letter)][:, CAPP * q:CAPP * q + CAPP]
+            dst = T["w%d%s" % (t + 1, letter)][:, lo:lo + CAPP]
+            if kind == "c":
+                src, dst = src.bitcast(dt.uint8), dst.bitcast(dt.uint8)
+            moves.append(RemoteDMATransfer(dst_ids=[DstId(rid=rid, pnc=pid)],
+                                           dma_engine_mask=sum(1 << e for e in part[d]),
+                                           remote_sem=sem["ar%s%d" % (kind, t)], src=src, dst=dst))
+        g.remote_dma_fused(moves, local_sem=sem.sent)
+        return sum(len(e) for e in part.values())
+
+    fills = {2: 1, 3: 4, 4: 7}
+    for t in L:
+        wq, ws = "w%dq" % (t + 1), "w%ds" % (t + 1)
+        end = BASE + t * SLOTS
+        g.wait_ge(sem["pc%d" % t], 1)
+        n_sent += send(t, "c")
+        g.wait_ge(sem["pp%d" % t], 1)
+        n_sent += send(t, "s")
+
+        lists = ((("a%dq" % t), ("a%ds" % t), 8 * (t - 1), "ac%d" % t, "as%d" % t),
+                 (("b%dq" % t), ("b%ds" % t), 24 + 8 * (t - 1), "bc%d" % t, "bs%d" % t))
+        ve.wait_ge(sem["fill%d" % (t + 1)], fills[t + 1])
+        ve.wait_ge(sem["arc%d" % t], expect_c)
+        for oq, os_, o, nc, ns in lists:
+            for h in (0, 1):
+                pick_codes(oq, 64 * h, 64 * h + 64, wq, 0, end, "lro", o + 4 * h, o + 4 * h + 4).then_inc(sem[nc], 1)
+        ve.wait_ge(sem["ars%d" % t], expect_s)
+        for oq, os_, o, nc, ns in lists:
+            pick_scales_v(os_, 64, 128, ws, 0, end, "lro", o + 4, o + 8).then_inc(sem[ns], 1)
+        sc.wait_ge(sem["fill%d" % (t + 1)], fills[t + 1])
+        sc.wait_ge(sem["ars%d" % t], expect_s)
+        for oq, os_, o, nc, ns in lists:
+            pick_scales_s(os_, 0, 64, ws, 0, end, "lro", o, o + 4).then_inc(sem[ns], 1)
+
+        for side, (oq, os_, o, nc, ns) in enumerate(lists):
+            te.wait_ge(sem[nc], 2)
+            te.wait_ge(sem[ns], 2)
+            for i in range(4):
+                w, s = ("wlq", "wls") if side == 0 else ("wrq", "wrs")
+                m = te.matmul_mx(T.ps[:, 512 * i:512 * i + P], T[w][:, 128 * i:128 * i + 128],
+                                 T[s][:, 128 * i:128 * i + 128], T[oq][:], T[os_][:], side == 0, side == 1)
+                if side == 1:
+                    m.then_inc(sem["m%d_%d" % (i, t)], 1)
+
+        h = T["h%d" % t]
+        for i in (0, 2):
+            sc.wait_ge(sem["m%d_%d" % (i, t)], 1)
+            sc.activation(h[:, i:4 * P:4], T.ps[:, 512 * i:512 * i + P], Relu, scale=0.05).then_inc(sem["ev%d" % t], 1)
+        for i in (1, 3):
+            ve.wait_ge(sem["m%d_%d" % (i, t)], 1)
+            ve.tensor_scalar(h[:, i:4 * P:4], T.ps[:, 512 * i:512 * i + P], 0.0, 0.05,
+                             AluOpType.max, AluOpType.mult).then_inc(sem["ev%d" % t], 1)
+        ve.wait_ge(sem["ev%d" % t], 4)
+        if t == 3:
+            break
+        lo = LEAVES + (t - 1) * P
+        ve.quantize_mx(T[wq][:, lo:lo + P], T[ws][:, lo:lo + P], h[:]).then_inc(sem["nd%d" % t], 1)
+
+        ve.wait_ge(sem["nd%d" % t], 1)
+        sc.wait_ge(sem["nd%d" % t], 1)
+        pick_codes("s%dq" % (t + 1), 0, 128, wq, 0, end, "sno", 8 * t, 8 * t + 8).then_inc(sem["pc%d" % (t + 1)], 1)
+        pick_scales_s("s%ds" % (t + 1), 0, 128, ws, 0, end, "sno", 8 * t, 8 * t + 8).then_inc(sem["pp%d" % (t + 1)], 1)
+
+        s0 = BASE + (t - 1) * SLOTS
+        for w in range(t + 2, 5):
+            f = sem["fill%d" % w]
+            nq, n_s = "w%dq" % w, "w%ds" % w
+            ve.quantize_mx(T[nq][:, lo:lo + P], T[n_s][:, lo:lo + P], h[:]).then_inc(f, 1)
+            pick_codes(nq, s0, s0 + SLOTS, wq, s0, s0 + SLOTS, "idu", 0, 8).then_inc(f, 1)
+            pick_scales_s(n_s, s0, s0 + SLOTS, ws, s0, s0 + SLOTS, "idu", 0, 8).then_inc(f, 1)
+
+    ve.quantize_mx(T.hq[:], T.hs[:], T.h3[:]).then_inc(sem.qh, 1)
+    te.wait_ge(sem.qh, 1)
+    te.matmul_mx(T.psy[:, 0:P], T.vq[:], T.vs[:], T.hq[:], T.hs[:], True, True).then_inc(sem.mmy, 1)
+    ve.wait_ge(sem.mmy, 1)
+    ve.tensor_copy(T.ysb[:], T.psy[:, 0:P]).then_inc(sem.ycp, 1)
+    sy.wait_ge(sem.ycp, 1)
+    sy.dma_start(T.y[:], T.ysb[:]).then_inc(sem.sty, 16)
+    sy.wait_ge(sem.sty, 16)
+    g.wait_ge(sem.sent, n_sent)

@@ -4,6 +4,7 @@ from concourse.mybir import dt, AluOpType, ActivationFunctionType
 N, LEAVES, P, CAPP = 8, 256, 128, 16
 BASE = LEAVES + 3 * P
 SLOTS = N * CAPP
+OUT = SLOTS - CAPP
 L = (1, 2, 3)
 
 SCRATCH = {
@@ -34,7 +35,7 @@ SCRATCH = {
     "ps": ("psum", [128, 2048], "float32"),
     "psy": ("psum", [128, 512], "float32"),
 }
-SEMAPHORES = ["ldx", "ldsn", "ldwl", "ldwr", "ldlr", "ldv", "csn", "clr", "q1", "qwl", "qwr", "qv",
+SEMAPHORES = ["ldx0", "ldx1", "ldsn", "ldwl", "ldwr", "ldlr", "ldv", "csn", "csm", "clr", "q1", "qwl", "qwr", "qv",
               "iot", "id1", "id2", "idf", "fill2", "fill3", "fill4", "sent", "qh", "mmy", "ycp", "sty"]
 for t in L:
     SCRATCH["w%dq" % (t + 1)] = ("sbuf", [128, BASE + t * SLOTS], "float8_e4m3fn_x4")
@@ -48,21 +49,23 @@ for t in L:
 
 
 def plan(src, cores, topo):
-    away = [d for d in cores if topo.chip(d) != topo.chip(src)]
-    home = [d for d in cores if topo.chip(d) == topo.chip(src) and d != src]
+    chip = topo.chip(src)
+    home = [d for d in cores if topo.chip(d) == chip and d != src]
+    away = [d for d in cores if topo.chip(d) != chip]
+    near = [d for d in away if topo.mates(chip, topo.chip(d)) or topo.same_plane(chip, topo.chip(d))]
+    far = [d for d in away if d not in near]
     off = topo.engines(src, away[0])
-    half = len(off) // 2
+    even, odd = off[0::2], off[1::2]
     codes, scales = {}, {}
-    for k, d in enumerate(away):
-        if k < 2:
-            codes[d] = off[2 * k:2 * k + 2]
-            scales[d] = off[half + 2 * k:half + 2 * k + 2]
-        else:
-            codes[d] = [off[half + k - 2]]
-            scales[d] = [off[k - 2]]
-    for k, d in enumerate(home):
-        own = [e for e in topo.engines(src, d) if e not in off]
-        codes[d] = scales[d] = own[2 * k:2 * k + 2]
+    for k, d in enumerate(far):
+        codes[d] = even[2 * k:2 * k + 2]
+        scales[d] = [even[k]]
+    for k, d in enumerate(near):
+        codes[d] = [odd[k]]
+        scales[d] = odd[2 * k:2 * k + 2] if k < 2 else [even[k]]
+    own = [e for e in topo.engines(src, home[0]) if e not in off]
+    for d in home:
+        codes[d] = scales[d] = [own[0], own[2]]
     return codes, scales
 
 
@@ -85,15 +88,16 @@ def rank_program(g, core, T, topo):
     def pick_scales_s(out, o0, o1, win, w0, w1, off, i0, i1):
         return sc.activation(T[out][:, o0:o1], T[win][:, w0:w1].indirect(T[off][:, i0:i1]), Copy)
 
-    sc.dma_start(T.xt[:], T.x[:]).then_inc(sem.ldx, 16)
+    half = 2 * LEAVES
+    sc.dma_start(T.xt[:, 0:half], T.x[:, 0:half]).then_inc(sem.ldx0, 16)
     for k in range(8):
-        (sy if k % 2 == 0 else sc).dma_start(T.sni[16 * k:16 * k + 16, :], T.sn[:]).then_inc(sem.ldsn, 16)
+        (sc if k < 4 else sy).dma_start(T.sni[16 * k:16 * k + 16, :], T.sn[:]).then_inc(sem.ldsn, 16)
+    sy.dma_start(T.xt[:, half:2 * half], T.x[:, half:2 * half]).then_inc(sem.ldx1, 16)
     sy.dma_start(T.wlt[:], T.wl[:]).then_inc(sem.ldwl, 16)
     sy.dma_start(T.wrt[:], T.wr[:]).then_inc(sem.ldwr, 16)
     for k in range(8):
         sy.dma_start(T.lri[16 * k:16 * k + 16, 0:24], T.lc[:]).then_inc(sem.ldlr, 16)
-        sy.dma_start(T.lri[16 * k:16 * k + 16, 24:48], T.rc[:]).then_inc(sem.ldlr, 16)
-    sy.dma_start(T.vt[:], T.v[:]).then_inc(sem.ldv, 16)
+        sc.dma_start(T.lri[16 * k:16 * k + 16, 24:48], T.rc[:]).then_inc(sem.ldlr, 16)
 
     g.iota(T.ida[:], [[0, 8]], 0, 1).then_inc(sem.iot, 1)
     n_iota = 1
@@ -102,18 +106,30 @@ def rank_program(g, core, T, topo):
             g.iota(T.idb[:, a:b], [[16, b - a]], base, 0).then_inc(sem.iot, 1)
             n_iota += 1
 
+    def cast_sn(t, done):
+        n = 0
+        for q0, q1, to in ((0, rank, 0), (rank + 1, N, rank)):
+            if q0 < q1:
+                c = 8 * (t - 1)
+                ve.tensor_copy(T.sno[:, c + to:c + to + q1 - q0], T.sni[:, c + q0:c + q1]).then_inc(done, 1)
+                n += 1
+        return n
+
+    ve.wait_ge(sem.ldx0, 16)
+    ve.quantize_mx(T.w1q[:, 0:P], T.w1s[:, 0:P], T.xt[:, 0:half]).then_inc(sem.q1, 1)
     ve.wait_ge(sem.ldsn, 128)
-    ve.tensor_copy(T.sno[:], T.sni[:]).then_inc(sem.csn, 1)
-    ve.wait_ge(sem.ldx, 16)
-    ve.quantize_mx(T.w1q[:], T.w1s[:], T.xt[:]).then_inc(sem.q1, 1)
-    ve.wait_ge(sem.csn, 1)
-    ve.wait_ge(sem.q1, 1)
-    pick_codes("s1q", 0, 128, "w1q", 0, LEAVES, "sno", 0, 8).then_inc(sem.pc1, 1)
-    sc.wait_ge(sem.csn, 1)
-    sc.wait_ge(sem.q1, 1)
-    pick_scales_s("s1s", 0, 128, "w1s", 0, LEAVES, "sno", 0, 8).then_inc(sem.pp1, 1)
+    n1 = cast_sn(1, sem.csn)
+    ve.wait_ge(sem.ldx1, 16)
+    ve.quantize_mx(T.w1q[:, P:LEAVES], T.w1s[:, P:LEAVES], T.xt[:, half:2 * half]).then_inc(sem.q1, 1)
+    ve.wait_ge(sem.csn, n1)
+    ve.wait_ge(sem.q1, 2)
+    pick_codes("s1q", 0, OUT, "w1q", 0, LEAVES, "sno", 0, 7).then_inc(sem.pc1, 1)
+    sc.wait_ge(sem.csn, n1)
+    sc.wait_ge(sem.q1, 2)
+    pick_scales_s("s1s", 0, OUT, "w1s", 0, LEAVES, "sno", 0, 7).then_inc(sem.pp1, 1)
 
     ve.quantize_mx(T.w2q[:, 0:LEAVES], T.w2s[:, 0:LEAVES], T.xt[:]).then_inc(sem.fill2, 1)
+    n2 = cast_sn(2, sem.csm) + cast_sn(3, sem.csm)
     ve.wait_ge(sem.iot, n_iota)
     ve.tensor_scalar(T.idc[:], T.ida[:], 15, None, AluOpType.bitwise_and).then_inc(sem.id1, 1)
     ve.wait_ge(sem.id1, 1)
@@ -126,17 +142,10 @@ def rank_program(g, core, T, topo):
     ve.quantize_mx(T.wrq[:], T.wrs[:], T.wrt[:]).then_inc(sem.qwr, 1)
     ve.wait_ge(sem.ldlr, 256)
     ve.tensor_copy(T.lro[:], T.lri[:]).then_inc(sem.clr, 1)
-    ve.quantize_mx(T.w3q[:, 0:LEAVES], T.w3s[:, 0:LEAVES], T.xt[:]).then_inc(sem.fill3, 1)
-    ve.quantize_mx(T.w4q[:, 0:LEAVES], T.w4s[:, 0:LEAVES], T.xt[:]).then_inc(sem.fill4, 1)
-    ve.wait_ge(sem.ldv, 16)
-    ve.quantize_mx(T.vq[:], T.vs[:], T.vt[:]).then_inc(sem.qv, 1)
-    ve.wait_ge(sem.clr, 1)
-    ve.wait_ge(sem.idf, 1)
-    sc.wait_ge(sem.clr, 1)
-    sc.wait_ge(sem.idf, 1)
-    te.wait_ge(sem.qwl, 1)
-    te.wait_ge(sem.qwr, 1)
-    te.wait_ge(sem.qv, 1)
+    for q in (ve, sc):
+        q.wait_ge(sem.csm, n2)
+        q.wait_ge(sem.idf, 1)
+        q.wait_ge(sem.clr, 1)
 
     plans = {c: plan(c, cores, topo) for c in cores}
     expect_c = sum(len(plans[c][0][core]) for c in cores if c != core)
@@ -149,6 +158,7 @@ def rank_program(g, core, T, topo):
         moves = []
         for d in sorted(part, key=lambda c: (topo.chip(c) == topo.chip(core), c)):
             q = T.rank_of(d)
+            q -= q > rank
             rid, pid, _ = topo.addr(d)
             src = T["s%d%s" % (t, letter)][:, CAPP * q:CAPP * q + CAPP]
             dst = T["w%d%s" % (t + 1, letter)][:, lo:lo + CAPP]
@@ -160,6 +170,9 @@ def rank_program(g, core, T, topo):
         g.remote_dma_fused(moves, local_sem=sem.sent)
         return sum(len(e) for e in part.values())
 
+    sy.wait_ge(sem.arc1, expect_c)
+    sy.dma_start(T.vt[:], T.v[:]).then_inc(sem.ldv, 16)
+
     fills = {2: 1, 3: 4, 4: 7}
     for t in L:
         wq, ws = "w%dq" % (t + 1), "w%ds" % (t + 1)
@@ -169,28 +182,38 @@ def rank_program(g, core, T, topo):
         g.wait_ge(sem["pp%d" % t], 1)
         n_sent += send(t, "s")
 
-        lists = ((("a%dq" % t), ("a%ds" % t), 8 * (t - 1), "ac%d" % t, "as%d" % t),
-                 (("b%dq" % t), ("b%ds" % t), 24 + 8 * (t - 1), "bc%d" % t, "bs%d" % t))
+        ac, as_, bc, bs = (sem["%s%d" % (n, t)] for n in ("ac", "as", "bc", "bs"))
+        aq, a_s, bq, b_s = "a%dq" % t, "a%ds" % t, "b%dq" % t, "b%ds" % t
+        oa, ob = 8 * (t - 1), 24 + 8 * (t - 1)
+        parts = 1 if t == 1 else 2
         ve.wait_ge(sem["fill%d" % (t + 1)], fills[t + 1])
         ve.wait_ge(sem["arc%d" % t], expect_c)
-        for oq, os_, o, nc, ns in lists:
-            for h in (0, 1):
-                pick_codes(oq, 64 * h, 64 * h + 64, wq, 0, end, "lro", o + 4 * h, o + 4 * h + 4).then_inc(sem[nc], 1)
-        ve.wait_ge(sem["ars%d" % t], expect_s)
-        for oq, os_, o, nc, ns in lists:
-            pick_scales_v(os_, 64, 128, ws, 0, end, "lro", o + 4, o + 8).then_inc(sem[ns], 1)
         sc.wait_ge(sem["fill%d" % (t + 1)], fills[t + 1])
         sc.wait_ge(sem["ars%d" % t], expect_s)
-        for oq, os_, o, nc, ns in lists:
-            pick_scales_s(os_, 0, 64, ws, 0, end, "lro", o, o + 4).then_inc(sem[ns], 1)
+        if t == 1:
+            pick_codes(aq, 0, 128, wq, 0, end, "lro", oa, oa + 8).then_inc(ac, 1)
+            pick_scales_s(a_s, 0, 128, ws, 0, end, "lro", oa, oa + 8).then_inc(as_, 1)
+            pick_codes(bq, 0, 128, wq, 0, end, "lro", ob, ob + 8).then_inc(bc, 1)
+            pick_scales_s(b_s, 0, 128, ws, 0, end, "lro", ob, ob + 8).then_inc(bs, 1)
+        else:
+            pick_codes(aq, 0, 64, wq, 0, end, "lro", oa, oa + 4).then_inc(ac, 1)
+            pick_codes(aq, 64, 128, wq, 0, end, "lro", oa + 4, oa + 8).then_inc(ac, 1)
+            ve.wait_ge(sem["ars%d" % t], expect_s)
+            pick_scales_v(a_s, 64, 128, ws, 0, end, "lro", oa + 4, oa + 8).then_inc(as_, 1)
+            pick_scales_s(a_s, 0, 64, ws, 0, end, "lro", oa, oa + 4).then_inc(as_, 1)
+            pick_codes(bq, 0, 128, wq, 0, end, "lro", ob, ob + 8).then_inc(bc, 1)
+            pick_scales_s(b_s, 0, 128, ws, 0, end, "lro", ob, ob + 8).then_inc(bs, 1)
 
-        for side, (oq, os_, o, nc, ns) in enumerate(lists):
-            te.wait_ge(sem[nc], 2)
-            te.wait_ge(sem[ns], 2)
+        for side in (0, 1):
+            if t == 1:
+                te.wait_ge(sem.qwl if side == 0 else sem.qwr, 1)
+            te.wait_ge(ac if side == 0 else bc, parts if side == 0 else 1)
+            te.wait_ge(as_ if side == 0 else bs, parts if side == 0 else 1)
+            w, s = ("wlq", "wls") if side == 0 else ("wrq", "wrs")
+            xq, xs = (aq, a_s) if side == 0 else (bq, b_s)
             for i in range(4):
-                w, s = ("wlq", "wls") if side == 0 else ("wrq", "wrs")
                 m = te.matmul_mx(T.ps[:, 512 * i:512 * i + P], T[w][:, 128 * i:128 * i + 128],
-                                 T[s][:, 128 * i:128 * i + 128], T[oq][:], T[os_][:], side == 0, side == 1)
+                                 T[s][:, 128 * i:128 * i + 128], T[xq][:], T[xs][:], side == 0, side == 1)
                 if side == 1:
                     m.then_inc(sem["m%d_%d" % (i, t)], 1)
 
@@ -198,6 +221,8 @@ def rank_program(g, core, T, topo):
         for i in (0, 2):
             sc.wait_ge(sem["m%d_%d" % (i, t)], 1)
             sc.activation(h[:, i:4 * P:4], T.ps[:, 512 * i:512 * i + P], Relu, scale=0.05).then_inc(sem["ev%d" % t], 1)
+        if t == 1:
+            ve.wait_ge(sem.ars1, expect_s)
         for i in (1, 3):
             ve.wait_ge(sem["m%d_%d" % (i, t)], 1)
             ve.tensor_scalar(h[:, i:4 * P:4], T.ps[:, 512 * i:512 * i + P], 0.0, 0.05,
@@ -210,18 +235,35 @@ def rank_program(g, core, T, topo):
 
         ve.wait_ge(sem["nd%d" % t], 1)
         sc.wait_ge(sem["nd%d" % t], 1)
-        pick_codes("s%dq" % (t + 1), 0, 128, wq, 0, end, "sno", 8 * t, 8 * t + 8).then_inc(sem["pc%d" % (t + 1)], 1)
-        pick_scales_s("s%ds" % (t + 1), 0, 128, ws, 0, end, "sno", 8 * t, 8 * t + 8).then_inc(sem["pp%d" % (t + 1)], 1)
+        pick_codes("s%dq" % (t + 1), 0, OUT, wq, 0, end, "sno", 8 * t, 8 * t + 7).then_inc(sem["pc%d" % (t + 1)], 1)
+        pick_scales_s("s%ds" % (t + 1), 0, OUT, ws, 0, end, "sno", 8 * t, 8 * t + 7).then_inc(sem["pp%d" % (t + 1)], 1)
 
-        s0 = BASE + (t - 1) * SLOTS
-        for w in range(t + 2, 5):
-            f = sem["fill%d" % w]
-            nq, n_s = "w%dq" % w, "w%ds" % w
-            ve.quantize_mx(T[nq][:, lo:lo + P], T[n_s][:, lo:lo + P], h[:]).then_inc(f, 1)
-            pick_codes(nq, s0, s0 + SLOTS, wq, s0, s0 + SLOTS, "idu", 0, 8).then_inc(f, 1)
-            pick_scales_s(n_s, s0, s0 + SLOTS, ws, s0, s0 + SLOTS, "idu", 0, 8).then_inc(f, 1)
+        def fill_leaves(w):
+            ve.quantize_mx(T["w%dq" % w][:, 0:LEAVES], T["w%ds" % w][:, 0:LEAVES], T.xt[:]).then_inc(sem["fill%d" % w], 1)
+
+        def fill_nodes(w):
+            ve.quantize_mx(T["w%dq" % w][:, lo:lo + P], T["w%ds" % w][:, lo:lo + P], h[:]).then_inc(sem["fill%d" % w], 1)
+
+        def fill_slots(w, u):
+            s0, s1 = BASE + (u - 1) * SLOTS, BASE + u * SLOTS
+            pick_codes("w%dq" % w, s0, s1, wq, s0, s1, "idu", 0, 8).then_inc(sem["fill%d" % w], 1)
+            pick_scales_s("w%ds" % w, s0, s1, ws, s0, s1, "idu", 0, 8).then_inc(sem["fill%d" % w], 1)
+
+        if t == 1:
+            fill_nodes(3)
+            fill_slots(3, 1)
+            fill_leaves(3)
+            fill_leaves(4)
+            fill_nodes(4)
+        else:
+            fill_nodes(4)
+            fill_slots(4, 1)
+            fill_slots(4, 2)
+            ve.wait_ge(sem.ldv, 16)
+            ve.quantize_mx(T.vq[:], T.vs[:], T.vt[:]).then_inc(sem.qv, 1)
 
     ve.quantize_mx(T.hq[:], T.hs[:], T.h3[:]).then_inc(sem.qh, 1)
+    te.wait_ge(sem.qv, 1)
     te.wait_ge(sem.qh, 1)
     te.matmul_mx(T.psy[:, 0:P], T.vq[:], T.vs[:], T.hq[:], T.hs[:], True, True).then_inc(sem.mmy, 1)
     ve.wait_ge(sem.mmy, 1)

from concourse.bass import DstId, RemoteDMATransfer
from concourse.mybir import dt, AluOpType, ActivationFunctionType

N, LEAVES, P, CAPP = 8, 256, 128, 16
BASE = LEAVES + 3 * P
SLOTS = N * CAPP
OUT = SLOTS - CAPP
L = (1, 2, 3)

SCRATCH = {
    "xt": ("sbuf", [128, 4 * LEAVES], "bfloat16"),
    "wlt": ("sbuf", [128, 2048], "bfloat16"),
    "wrt": ("sbuf", [128, 2048], "bfloat16"),
    "vt": ("sbuf", [128, 512], "bfloat16"),
    "wlq": ("sbuf", [128, 512], "float8_e4m3fn_x4"),
    "wls": ("sbuf", [128, 512], "uint8"),
    "wrq": ("sbuf", [128, 512], "float8_e4m3fn_x4"),
    "wrs": ("sbuf", [128, 512], "uint8"),
    "vq": ("sbuf", [128, 128], "float8_e4m3fn_x4"),
    "vs": ("sbuf", [128, 128], "uint8"),
    "sni": ("sbuf", [128, 24], "int32"),
    "sno": ("sbuf", [128, 24], "uint16"),
    "lri": ("sbuf", [128, 48], "int32"),
    "lro": ("sbuf", [128, 48], "uint16"),
    "ida": ("sbuf", [128, 8], "int32"),
    "idb": ("sbuf", [128, 8], "int32"),
    "idc": ("sbuf", [128, 8], "int32"),
    "idd": ("sbuf", [128, 8], "int32"),
    "idu": ("sbuf", [128, 8], "uint16"),
    "w1q": ("sbuf", [128, LEAVES], "float8_e4m3fn_x4"),
    "w1s": ("sbuf", [128, LEAVES], "uint8"),
    "hq": ("sbuf", [128, P], "float8_e4m3fn_x4"),
    "hs": ("sbuf", [128, P], "uint8"),
    "ysb": ("sbuf", [128, P], "float32"),
    "ps": ("psum", [128, 2048], "float32"),
    "psy": ("psum", [128, 512], "float32"),
}
SEMAPHORES = ["ldx0", "ldx1", "ldsn", "ldwl", "ldwr", "ldlr", "ldv", "csn", "csm", "clr", "q1", "qwl", "qwr", "qv",
              "iot", "id1", "id2", "idf", "fill2", "fill3", "fill4", "sent", "qh", "mmy", "ycp", "sty"]
for t in L:
    SCRATCH["w%dq" % (t + 1)] = ("sbuf", [128, BASE + t * SLOTS], "float8_e4m3fn_x4")
    SCRATCH["w%ds" % (t + 1)] = ("sbuf", [128, BASE + t * SLOTS], "uint8")
    for b in ("s", "a", "b"):
        SCRATCH["%s%dq" % (b, t)] = ("sbuf", [128, 128], "float8_e4m3fn_x4")
        SCRATCH["%s%ds" % (b, t)] = ("sbuf", [128, 128], "uint8")
    SCRATCH["h%d" % t] = ("sbuf", [128, 4 * P], "bfloat16")
    SEMAPHORES += ["%s%d" % (n, t) for n in ("pc", "pp", "arc", "ars", "ac", "as", "bc", "bs",
                                             "m0_", "m1_", "m2_", "m3_", "ev", "nd")]


def plan(src, cores, topo):
    chip = topo.chip(src)
    home = [d for d in cores if topo.chip(d) == chip and d != src]
    away = [d for d in cores if topo.chip(d) != chip]
    near = [d for d in away if topo.mates(chip, topo.chip(d)) or topo.same_plane(chip, topo.chip(d))]
    far = [d for d in away if d not in near]
    off = topo.engines(src, away[0])
    even, odd = off[0::2], off[1::2]
    codes, scales = {}, {}
    for k, d in enumerate(far):
        codes[d] = even[2 * k:2 * k + 2]
        scales[d] = [even[k]]
    for k, d in enumerate(near):
        codes[d] = [odd[k]]
        scales[d] = odd[2 * k:2 * k + 2] if k < 2 else [even[k]]
    own = [e for e in topo.engines(src, home[0]) if e not in off]
    for d in home:
        codes[d] = scales[d] = [own[0], own[2]]
    return codes, scales


def rank_program(g, core, T, topo):
    rank = T.rank_of(core)
    if rank is None:
        return
    cores = list(T.cores)
    sem = T.sem
    ve, sc, te, sy = g.vector, g.scalar, g.tensor, g.sync
    Copy, Relu = ActivationFunctionType.Copy, ActivationFunctionType.Relu

    def pick_codes(out, o0, o1, win, w0, w1, off, i0, i1):
        return ve.tensor_copy(T[out][:, o0:o1].bitcast(dt.uint32),
                              T[win][:, w0:w1].bitcast(dt.uint32).indirect(T[off][:, i0:i1]))

    def pick_scales_v(out, o0, o1, win, w0, w1, off, i0, i1):
        return ve.tensor_copy(T[out][:, o0:o1], T[win][:, w0:w1].indirect(T[off][:, i0:i1]))

    def pick_scales_s(out, o0, o1, win, w0, w1, off, i0, i1):
        return sc.activation(T[out][:, o0:o1], T[win][:, w0:w1].indirect(T[off][:, i0:i1]), Copy)

    half = 2 * LEAVES
    sc.dma_start(T.xt[:, 0:half], T.x[:, 0:half]).then_inc(sem.ldx0, 16)
    for k in range(8):
        (sc if k < 4 else sy).dma_start(T.sni[16 * k:16 * k + 16, :], T.sn[:]).then_inc(sem.ldsn, 16)
    sy.dma_start(T.xt[:, half:2 * half], T.x[:, half:2 * half]).then_inc(sem.ldx1, 16)
    sy.dma_start(T.wlt[:], T.wl[:]).then_inc(sem.ldwl, 16)
    sy.dma_start(T.wrt[:], T.wr[:]).then_inc(sem.ldwr, 16)
    for k in range(8):
        sy.dma_start(T.lri[16 * k:16 * k + 16, 0:24], T.lc[:]).then_inc(sem.ldlr, 16)
        sc.dma_start(T.lri[16 * k:16 * k + 16, 24:48], T.rc[:]).then_inc(sem.ldlr, 16)

    g.iota(T.ida[:], [[0, 8]], 0, 1).then_inc(sem.iot, 1)
    n_iota = 1
    for a, b, base in ((0, rank, 0), (rank, rank + 1, 16 * ((rank + 1) % N)), (rank + 1, N, 16 * (rank + 1))):
        if a < b:
            g.iota(T.idb[:, a:b], [[16, b - a]], base, 0).then_inc(sem.iot, 1)
            n_iota += 1

    def cast_sn(t, done):
        n = 0
        for q0, q1, to in ((0, rank, 0), (rank + 1, N, rank)):
            if q0 < q1:
                c = 8 * (t - 1)
                ve.tensor_copy(T.sno[:, c + to:c + to + q1 - q0], T.sni[:, c + q0:c + q1]).then_inc(done, 1)
                n += 1
        return n

    ve.wait_ge(sem.ldx0, 16)
    ve.quantize_mx(T.w1q[:, 0:P], T.w1s[:, 0:P], T.xt[:, 0:half]).then_inc(sem.q1, 1)
    ve.wait_ge(sem.ldsn, 128)
    n1 = cast_sn(1, sem.csn)
    ve.wait_ge(sem.ldx1, 16)
    ve.quantize_mx(T.w1q[:, P:LEAVES], T.w1s[:, P:LEAVES], T.xt[:, half:2 * half]).then_inc(sem.q1, 1)
    ve.wait_ge(sem.csn, n1)
    ve.wait_ge(sem.q1, 2)
    pick_codes("s1q", 0, OUT, "w1q", 0, LEAVES, "sno", 0, 7).then_inc(sem.pc1, 1)
    sc.wait_ge(sem.csn, n1)
    sc.wait_ge(sem.q1, 2)
    pick_scales_s("s1s", 0, OUT, "w1s", 0, LEAVES, "sno", 0, 7).then_inc(sem.pp1, 1)

    ve.quantize_mx(T.w2q[:, 0:LEAVES], T.w2s[:, 0:LEAVES], T.xt[:]).then_inc(sem.fill2, 1)
    n2 = cast_sn(2, sem.csm) + cast_sn(3, sem.csm)
    ve.wait_ge(sem.iot, n_iota)
    ve.tensor_scalar(T.idc[:], T.ida[:], 15, None, AluOpType.bitwise_and).then_inc(sem.id1, 1)
    ve.wait_ge(sem.id1, 1)
    ve.tensor_tensor(T.idd[:], T.idc[:], T.idb[:], AluOpType.add).then_inc(sem.id2, 1)
    ve.wait_ge(sem.id2, 1)
    ve.tensor_copy(T.idu[:], T.idd[:]).then_inc(sem.idf, 1)
    ve.wait_ge(sem.ldwl, 16)
    ve.quantize_mx(T.wlq[:], T.wls[:], T.wlt[:]).then_inc(sem.qwl, 1)
    ve.wait_ge(sem.ldwr, 16)
    ve.quantize_mx(T.wrq[:], T.wrs[:], T.wrt[:]).then_inc(sem.qwr, 1)
    ve.wait_ge(sem.ldlr, 256)
    ve.tensor_copy(T.lro[:], T.lri[:]).then_inc(sem.clr, 1)
    for q in (ve, sc):
        q.wait_ge(sem.csm, n2)
        q.wait_ge(sem.idf, 1)
        q.wait_ge(sem.clr, 1)

    plans = {c: plan(c, cores, topo) for c in cores}
    expect_c = sum(len(plans[c][0][core]) for c in cores if c != core)
    expect_s = sum(len(plans[c][1][core]) for c in cores if c != core)
    n_sent = 0

    def send(t, kind):
        part, letter = plans[core][0 if kind == "c" else 1], "q" if kind == "c" else "s"
        lo = BASE + ((t - 1) * N + rank) * CAPP
        moves = []
        for d in sorted(part, key=lambda c: (topo.chip(c) == topo.chip(core), c)):
            q = T.rank_of(d)
            q -= q > rank
            rid, pid, _ = topo.addr(d)
            src = T["s%d%s" % (t, letter)][:, CAPP * q:CAPP * q + CAPP]
            dst = T["w%d%s" % (t + 1, letter)][:, lo:lo + CAPP]
            if kind == "c":
                src, dst = src.bitcast(dt.uint8), dst.bitcast(dt.uint8)
            moves.append(RemoteDMATransfer(dst_ids=[DstId(rid=rid, pnc=pid)],
                                           dma_engine_mask=sum(1 << e for e in part[d]),
                                           remote_sem=sem["ar%s%d" % (kind, t)], src=src, dst=dst))
        g.remote_dma_fused(moves, local_sem=sem.sent)
        return sum(len(e) for e in part.values())

    sy.wait_ge(sem.arc1, expect_c)
    sy.dma_start(T.vt[:], T.v[:]).then_inc(sem.ldv, 16)

    fills = {2: 1, 3: 4, 4: 7}
    for t in L:
        wq, ws = "w%dq" % (t + 1), "w%ds" % (t + 1)
        end = BASE + t * SLOTS
        g.wait_ge(sem["pc%d" % t], 1)
        n_sent += send(t, "c")
        g.wait_ge(sem["pp%d" % t], 1)
        n_sent += send(t, "s")

        ac, as_, bc, bs = (sem["%s%d" % (n, t)] for n in ("ac", "as", "bc", "bs"))
        aq, a_s, bq, b_s = "a%dq" % t, "a%ds" % t, "b%dq" % t, "b%ds" % t
        oa, ob = 8 * (t - 1), 24 + 8 * (t - 1)
        parts = 1 if t == 1 else 2
        ve.wait_ge(sem["fill%d" % (t + 1)], fills[t + 1])
        ve.wait_ge(sem["arc%d" % t], expect_c)
        sc.wait_ge(sem["fill%d" % (t + 1)], fills[t + 1])
        sc.wait_ge(sem["ars%d" % t], expect_s)
        if t == 1:
            pick_codes(aq, 0, 128, wq, 0, end, "lro", oa, oa + 8).then_inc(ac, 1)
            pick_scales_s(a_s, 0, 128, ws, 0, end, "lro", oa, oa + 8).then_inc(as_, 1)
            pick_codes(bq, 0, 128, wq, 0, end, "lro", ob, ob + 8).then_inc(bc, 1)
            pick_scales_s(b_s, 0, 128, ws, 0, end, "lro", ob, ob + 8).then_inc(bs, 1)
        else:
            pick_codes(aq, 0, 64, wq, 0, end, "lro", oa, oa + 4).then_inc(ac, 1)
            pick_codes(aq, 64, 128, wq, 0, end, "lro", oa + 4, oa + 8).then_inc(ac, 1)
            ve.wait_ge(sem["ars%d" % t], expect_s)
            pick_scales_v(a_s, 64, 128, ws, 0, end, "lro", oa + 4, oa + 8).then_inc(as_, 1)
            pick_scales_s(a_s, 0, 64, ws, 0, end, "lro", oa, oa + 4).then_inc(as_, 1)
            pick_codes(bq, 0, 128, wq, 0, end, "lro", ob, ob + 8).then_inc(bc, 1)
            pick_scales_s(b_s, 0, 128, ws, 0, end, "lro", ob, ob + 8).then_inc(bs, 1)

        for side in (0, 1):
            if t == 1:
                te.wait_ge(sem.qwl if side == 0 else sem.qwr, 1)
            te.wait_ge(ac if side == 0 else bc, parts if side == 0 else 1)
            te.wait_ge(as_ if side == 0 else bs, parts if side == 0 else 1)
            w, s = ("wlq", "wls") if side == 0 else ("wrq", "wrs")
            xq, xs = (aq, a_s) if side == 0 else (bq, b_s)
            for i in range(4):
                m = te.matmul_mx(T.ps[:, 512 * i:512 * i + P], T[w][:, 128 * i:128 * i + 128],
                                 T[s][:, 128 * i:128 * i + 128], T[xq][:], T[xs][:], side == 0, side == 1)
                if side == 1:
                    m.then_inc(sem["m%d_%d" % (i, t)], 1)

        h = T["h%d" % t]
        for i in (0, 2):
            sc.wait_ge(sem["m%d_%d" % (i, t)], 1)
            sc.activation(h[:, i:4 * P:4], T.ps[:, 512 * i:512 * i + P], Relu, scale=0.05).then_inc(sem["ev%d" % t], 1)
        if t == 1:
            ve.wait_ge(sem.ars1, expect_s)
        for i in (1, 3):
            ve.wait_ge(sem["m%d_%d" % (i, t)], 1)
            ve.tensor_scalar(h[:, i:4 * P:4], T.ps[:, 512 * i:512 * i + P], 0.0, 0.05,
                             AluOpType.max, AluOpType.mult).then_inc(sem["ev%d" % t], 1)
        ve.wait_ge(sem["ev%d" % t], 4)
        if t == 3:
            break
        lo = LEAVES + (t - 1) * P
        ve.quantize_mx(T[wq][:, lo:lo + P], T[ws][:, lo:lo + P], h[:]).then_inc(sem["nd%d" % t], 1)

        ve.wait_ge(sem["nd%d" % t], 1)
        sc.wait_ge(sem["nd%d" % t], 1)
        pick_codes("s%dq" % (t + 1), 0, OUT, wq, 0, end, "sno", 8 * t, 8 * t + 7).then_inc(sem["pc%d" % (t + 1)], 1)
        pick_scales_s("s%ds" % (t + 1), 0, OUT, ws, 0, end, "sno", 8 * t, 8 * t + 7).then_inc(sem["pp%d" % (t + 1)], 1)

        def fill_leaves(w):
            ve.quantize_mx(T["w%dq" % w][:, 0:LEAVES], T["w%ds" % w][:, 0:LEAVES], T.xt[:]).then_inc(sem["fill%d" % w], 1)

        def fill_nodes(w):
            ve.quantize_mx(T["w%dq" % w][:, lo:lo + P], T["w%ds" % w][:, lo:lo + P], h[:]).then_inc(sem["fill%d" % w], 1)

        def fill_slots(w, u):
            s0, s1 = BASE + (u - 1) * SLOTS, BASE + u * SLOTS
            pick_codes("w%dq" % w, s0, s1, wq, s0, s1, "idu", 0, 8).then_inc(sem["fill%d" % w], 1)
            pick_scales_s("w%ds" % w, s0, s1, ws, s0, s1, "idu", 0, 8).then_inc(sem["fill%d" % w], 1)

        if t == 1:
            fill_nodes(3)
            fill_slots(3, 1)
            fill_leaves(3)
            fill_leaves(4)
            fill_nodes(4)
        else:
            fill_nodes(4)
            fill_slots(4, 1)
            fill_slots(4, 2)
            ve.wait_ge(sem.ldv, 16)
            ve.quantize_mx(T.vq[:], T.vs[:], T.vt[:]).then_inc(sem.qv, 1)

    ve.quantize_mx(T.hq[:], T.hs[:], T.h3[:]).then_inc(sem.qh, 1)
    te.wait_ge(sem.qv, 1)
    te.wait_ge(sem.qh, 1)
    te.matmul_mx(T.psy[:, 0:P], T.vq[:], T.vs[:], T.hq[:], T.hs[:], True, True).then_inc(sem.mmy, 1)
    ve.wait_ge(sem.mmy, 1)
    ve.tensor_copy(T.ysb[:], T.psy[:, 0:P]).then_inc(sem.ycp, 1)
    sy.wait_ge(sem.ycp, 1)
    sy.dma_start(T.y[:], T.ysb[:]).then_inc(sem.sty, 16)
    sy.wait_ge(sem.sty, 16)
    g.wait_ge(sem.sent, n_sent)
